import numpy as np
import ml_dtypes


def mxq(x, axis, fmt="e4m3"):
    dtype, down = {"e4m3": (ml_dtypes.float8_e4m3fn, 7), "e5m2": (ml_dtypes.float8_e5m2, 14)}[fmt]
    v = np.moveaxis(np.asarray(x, np.float32).astype(ml_dtypes.bfloat16).astype(np.float64), axis, -1)
    blocks = v.reshape(v.shape[:-1] + (-1, 32))
    amax = np.abs(blocks).max(-1, keepdims=True)
    byte = np.maximum(np.where(amax > 0, np.frexp(amax)[1] - 1 + 127, 0) - down, 1)
    scale = np.exp2(byte - 127.0)
    codes = (blocks / scale).astype(np.float32).astype(dtype).astype(np.float64)
    return np.moveaxis((codes * scale).reshape(v.shape), -1, axis)


WIDE = False


def mx_kscale(k):
    if not WIDE:
        return np.ones(k)
    levels = np.array([10, -10, 5, -5, 0])
    if k % 512:
        return np.exp2(np.random.permutation(np.resize(levels, k // 32))).repeat(32)
    a = np.empty((k // 512, 16))
    for p in range(k // 512):
        a[p, :8] = np.random.permutation(np.resize(levels, 8))
        for g in range(8):
            far = levels[np.abs(levels - a[p, g]) >= 10]
            a[p, g + 8] = far[np.random.randint(len(far))]
    return np.exp2(a.ravel()).repeat(32)


def f64(x):
    return np.asarray(x).astype(np.float64)


def striped(idx):
    return np.tile(idx.reshape(-1, 16).T, (8, 1)).astype(np.uint16)


def unstriped(offs):
    return offs[:16].T.reshape(-1).astype(np.int64)


def striped8(idx):
    return np.concatenate([x.reshape(-1, 16).T for x in idx]).astype(np.uint16)


def runs(offs, k):
    lists = np.stack([offs[16 * r : 16 * r + 16].T.reshape(-1) for r in range(8)]).astype(np.int64)
    return lists[np.arange(k) % 512 // 64]


def pack_weight(w):
    k, n = w.shape
    w = f64(np.asarray(w, np.float32).astype(ml_dtypes.bfloat16)).reshape(k // 32, 32, n)
    amax = np.abs(w).max(1)
    byte = np.clip(np.where(amax > 0, np.frexp(amax)[1] - 1 + 127 - 7, 1), 1, 254)
    scaled = (w * np.exp2(127.0 - byte)[:, None, :]).reshape(k, n).astype(np.float32)
    words = np.ascontiguousarray(scaled.reshape(k // 512, 128, 4, n).transpose(0, 1, 3, 2)).astype(ml_dtypes.float8_e4m3fn).view(np.uint8)
    return words, np.ascontiguousarray(byte.astype(np.uint8).reshape(k // 512, 16, n))


def unpack_weight(words, scales):
    g, p, n, _ = words.shape
    vals = np.ascontiguousarray(words).view(ml_dtypes.float8_e4m3fn).astype(np.float64) * np.repeat(np.exp2(scales.astype(np.float64) - 127.0), 8, axis=1)[..., None]
    return vals.transpose(0, 1, 3, 2).reshape(g * 512, n)


E2M1 = np.array([0.0, 0.5, 1.0, 1.5, 2.0, 3.0, 4.0, 6.0, -0.0, -0.5, -1.0, -1.5, -2.0, -3.0, -4.0, -6.0])


def pack_fp4(w):
    k, n = w.shape
    w = f64(np.asarray(w, np.float32).astype(ml_dtypes.bfloat16)).reshape(k // 32, 32, n)
    amax = np.abs(w).max(1)
    mant, ex = np.frexp(amax / 6.0)
    byte = np.clip(np.where(amax > 0, np.where(mant > 0.5, ex, ex - 1) + 127, 1), 1, 254)
    scaled = (w * np.exp2(127.0 - byte)[:, None, :]).reshape(k, n).astype(np.float32)
    c = np.ascontiguousarray(scaled.reshape(k // 512, 128, 4, n).transpose(0, 1, 3, 2)).astype(ml_dtypes.float4_e2m1fn).view(np.uint8) & 0xF
    words = (c[..., 0::2] | (c[..., 1::2] << 4)).reshape(k // 512, 128, 2 * n)
    return np.ascontiguousarray(words), np.ascontiguousarray(byte.astype(np.uint8).reshape(k // 512, 16, n))


def unpack_fp4(words, scales):
    g, _, n = scales.shape
    words = np.ascontiguousarray(words).reshape(g, 128, n, 2)
    nib = np.empty((g, 128, n, 4), np.uint8)
    nib[..., 0::2] = words & 0xF
    nib[..., 1::2] = words >> 4
    vals = E2M1[nib] * np.repeat(np.exp2(scales.astype(np.float64) - 127.0), 8, axis=1)[..., None]
    return vals.transpose(0, 1, 3, 2).reshape(g * 512, n)


def sigmoid(v):
    return 1.0 / (1.0 + np.exp(-np.maximum(v, -700.0)))


K, T, S, H, G, U = 512, 2048, 256, 512, 2048, 512


def setup_inputs():
    n = np.random.standard_normal
    s = mx_kscale(K)[:, None]
    packed_xT = pack_weight(n((K, T)) * s)
    packed_w1 = pack_fp4(n((K, H)) / np.sqrt(K) / s)
    packed_dT = pack_weight(n((K, G)) / s)
    perm = np.random.permutation(U)
    return {
        "x_words": packed_xT[0],
        "x_scales": packed_xT[1],
        "w1_words": packed_w1[0],
        "w1_scales": packed_w1[1],
        "sl": np.random.uniform(1.0, 2.0, (H, 1)).astype(np.float32),
        "th": (0.5 * n((H, 1))).astype(np.float32),
        "gs": (np.random.uniform(0.5, 1.5, (K, 1)) * s).astype(np.float32),
        "d_words": packed_dT[0],
        "d_scales": packed_dT[1],
        "offs": striped8(np.random.randint(0, T, (8, S))),
        "n1": striped(np.random.permutation(S)),
        "ka": striped8(np.random.randint(0, G, (8, H))),
        "kb": striped8(np.random.randint(0, G, (8, H))),
        "n2": striped(perm[:S]),
        "n3": striped(perm[S:]),
        "n4": striped(np.random.permutation(S)),
    }


def reference(x_words, x_scales, w1_words, w1_scales, sl, th, gs, d_words, d_scales, offs, n1, ka, kb, n2, n3, n4):
    d_ka = unpack_weight(d_words, d_scales)[np.arange(K)[:, None], runs(ka, K)]
    xq = unpack_weight(x_words, x_scales)[np.arange(K)[:, None], runs(offs, K)]
    y = unpack_fp4(w1_words, w1_scales).T @ xq
    sg = sigmoid(f64(sl) * (y[:, unstriped(n1)] - f64(th)))
    z = f64(gs) * (y * sg)
    zq = mxq(z, 0, "e4m3")
    d_kb = unpack_weight(d_words, d_scales)[np.arange(K)[:, None], runs(kb, K)]
    h = 0.0625 * (d_ka.T @ zq + d_kb.T @ zq)
    nw = h - h[:, unstriped(n4)]
    ph = np.zeros((H, U))
    ph[:, unstriped(n2)] = h
    out = ph.copy()
    out[:, unstriped(n3)] = nw
    return out

@@ -1,0 +1,236 @@
+from contextlib import ExitStack
+
+import concourse.mybir as mybir
+
+K, T, S, H, G, U = 512, 2048, 256, 512, 2048, 512
+FLOPS = 2 * K * H * S * 3
+
+F32 = mybir.dt.float32
+BF16 = mybir.dt.bfloat16
+I32 = mybir.dt.int32
+U32 = mybir.dt.uint32
+U16 = mybir.dt.uint16
+U8 = mybir.dt.uint8
+FP8X4 = mybir.dt.float8_e4m3fn_x4
+FP4X4 = mybir.dt.float4_e2m1fn_x4
+ACT = mybir.ActivationFunctionType
+MULT = mybir.AluOpType.mult
+SUBTRACT = mybir.AluOpType.subtract
+
+P = 128
+PACK = 4
+TILES = H // P
+HALF = S // 2
+PIECE = 256
+STRIPE = 16
+
+
+def entries(offsets, first, count):
+    return offsets[:, first // STRIPE : (first + count) // STRIPE]
+
+
+def place_scale_rows(queue, plane):
+    rows = plane[:].bitcast(I32)
+    for j in range(1, 4):
+        queue.dma_start(out=rows[j:P:32, :], in_=rows[8 * j : P : 32, :])
+
+
+def tile_picked_hdaqesapagq_none_p_kernel(
+    tc, x_words, x_scales, w1_words, w1_scales, sl, th, gs, d_words, d_scales, offs, n1, ka, kb, n2, n3, n4, out
+):
+    nc = tc.nc
+    with ExitStack() as ctx:
+        keep = ctx.enter_context(tc.tile_pool(name="keep", bufs=1))
+        psum = ctx.enter_context(tc.psum_pool(name="psum", bufs=1))
+
+        def load_list(source, name):
+            offsets = keep.tile(list(source.shape), U16, name=name)
+            nc.sync.dma_start(offsets[:], source)
+            return offsets
+
+        def load_words(source, name, tag):
+            words = keep.tile([P, source.shape[2]], I32, name=name, tag=tag, align_bytes=64)
+            nc.scalar.dma_start(out=words[:], in_=source[0].rearrange("p n r -> p (n r)").bitcast(I32))
+            return words
+
+        def load_rowwise(queue, source, name):
+            values = keep.tile([P, PACK], F32, name=name)
+            queue.dma_start(out=values[:], in_=source.rearrange("(p t) o -> p (t o)", t=PACK))
+            return values
+
+        offs_list = load_list(offs, "offs_list")
+        x_bytes = keep.tile([P, T], U8, name="x_bytes")
+        nc.scalar.dma_start(
+            out=x_bytes[:].bitcast(I32), in_=x_scales[0].bitcast(I32).unsqueeze(1).broadcast_to([16, 8, T // 4])
+        )
+        w1_bytes = keep.tile([P, H], U8, name="w1_bytes")
+        for q in range(4):
+            rows = w1_scales[0].bitcast(I32)[4 * q : 4 * q + 4, :]
+            nc.sync.dma_start(
+                out=w1_bytes[:].bitcast(I32)[32 * q : 32 * (q + 1), :], in_=rows.unsqueeze(0).broadcast_to([8, 4, H // 4])
+            )
+        x_table = load_words(x_words, "x_table", "x_table")
+        w1_raw = keep.tile([P, 2 * H], U8, name="w1_raw")
+        nc.sync.dma_start(out=w1_raw[:].bitcast(I32), in_=w1_words[0].bitcast(I32))
+
+        th_rows = load_rowwise(nc.gpsimd, th, "th_rows")
+        d_bytes = keep.tile([P, G], U8, name="d_bytes")
+        nc.vector.memset(d_bytes[:].bitcast(I32), 0)
+        nc.gpsimd.dma_start(out=d_bytes[:].bitcast(I32)[0:P:8, :], in_=d_scales[0].bitcast(I32))
+        sl_rows = load_rowwise(nc.gpsimd, sl, "sl_rows")
+        gs_rows = load_rowwise(nc.gpsimd, gs, "gs_rows")
+
+        code_lists = [load_list(ka, "ka_list"), load_list(kb, "kb_list")]
+        n1_list = load_list(n1, "n1_list")
+        n2_list = load_list(n2, "n2_list")
+        n4_list = load_list(n4, "n4_list")
+        n3_list = load_list(n3, "n3_list")
+
+        x_picked = keep.tile([P, S], U8, name="x_picked", tag="d_table", align_bytes=64)
+        nc.vector.tensor_copy(out=x_picked[:], in_=x_bytes[:].indirect(offs_list[:]))
+        x_plane = keep.tile([P, S], U8, name="x_plane", align_bytes=64)
+        nc.vector.tensor_copy(out=x_plane[:].bitcast(I32), in_=x_picked[:].bitcast(I32))
+        place_scale_rows(nc.scalar, x_plane)
+        d_table = load_words(d_words, "d_table", "d_table")
+
+        w1_plane = keep.tile([P, H], U8, name="w1_plane", align_bytes=64)
+        nc.vector.tensor_copy(
+            out=w1_plane[:].rearrange("p (t m) -> p t m", t=PACK), in_=w1_bytes[:].rearrange("p (m t) -> p t m", t=PACK)
+        )
+        w1_codes = keep.tile([P, 2 * H], U8, name="w1_codes", align_bytes=64)
+        nc.scalar.copy(
+            out=w1_codes[:].bitcast(U16).rearrange("p (t m) -> p t m", t=PACK),
+            in_=w1_raw[:].bitcast(U16).rearrange("p (m t) -> p t m", t=PACK),
+        )
+        bias = keep.tile([P, PACK], F32, name="bias")
+        nc.vector.scalar_tensor_tensor(out=bias[:], in0=th_rows[:], scalar=-1.0, in1=sl_rows[:], op0=MULT, op1=MULT)
+
+        x_codes = keep.tile([P, S], U32, name="x_codes", align_bytes=64)
+        nc.vector.tensor_copy(out=x_codes[:], in_=x_table[:].bitcast(U32).indirect(offs_list[:]))
+
+        d_planes = [keep.tile([P, 2 * PIECE], U8, name=f"d_plane{piece}", align_bytes=64) for piece in range(2)]
+
+        def pick_d_scales(piece, c, tag):
+            picked = keep.tile([P, PIECE], U8, name=f"d_picked{piece}_{c}", tag=tag, align_bytes=64)
+            nc.vector.tensor_copy(out=picked[:], in_=d_bytes[:].indirect(entries(code_lists[c], piece * PIECE, PIECE)))
+            nc.vector.tensor_copy(
+                out=d_planes[piece][:, c * PIECE : (c + 1) * PIECE].bitcast(I32), in_=picked[:].bitcast(I32)
+            )
+
+        def pick_d_words(piece, tag):
+            codes = keep.tile([P, 2 * PIECE], U32, name=f"d_codes{piece}", tag=tag, align_bytes=64)
+            for c, code_list in enumerate(code_lists):
+                nc.vector.tensor_copy(
+                    out=codes[:, c * PIECE : (c + 1) * PIECE],
+                    in_=d_table[:].bitcast(U32).indirect(entries(code_list, piece * PIECE, PIECE)),
+                )
+            return codes
+
+        pick_d_scales(0, 0, "d_picked")
+        pick_d_scales(0, 1, "x_table")
+        place_scale_rows(nc.sync, d_planes[0])
+
+        y = []
+        for t in range(TILES):
+            y_bank = psum.tile([P, S], F32, name=f"y_bank{t}", tag=f"bank{t}")
+            nc.tensor.matmul_mx(
+                out=y_bank[:],
+                lhsT=w1_codes[:, 2 * P * t : 2 * P * (t + 1)].bitcast(FP4X4),
+                lhsT_scale=w1_plane[:, P * t : P * (t + 1)],
+                rhs=x_codes[:].bitcast(FP8X4),
+                rhs_scale=x_plane[:],
+                start=True,
+                stop=True,
+            )
+            y_tile = keep.tile([P, S], F32, name=f"y{t}")
+            nc.vector.tensor_copy(out=y_tile[:], in_=y_bank[:])
+            y.append(y_tile)
+
+        z_codes = keep.tile([P, S], U32, name="z_codes", align_bytes=64)
+        z_plane = keep.tile([P, S], U8, name="z_plane", align_bytes=64)
+
+        def quantise_z(half):
+            cols = slice(half * HALF, (half + 1) * HALF)
+            z_rows = keep.tile([P, PACK, HALF], BF16, name=f"z_rows{half}")
+            for t in range(TILES):
+                sg = keep.tile([P, HALF], F32, name=f"sg{half}_{t}")
+                nc.scalar.activation(
+                    out=sg[:],
+                    in_=y[t][:].indirect(entries(n1_list, half * HALF, HALF)),
+                    func=ACT.Sigmoid,
+                    scale=sl_rows[:, t : t + 1],
+                    bias=bias[:, t : t + 1],
+                )
+                nc.vector.scalar_tensor_tensor(
+                    out=z_rows[:, t, :], in0=y[t][:, cols], scalar=gs_rows[:, t : t + 1], in1=sg[:], op0=MULT, op1=MULT
+                )
+            z_grouped = keep.tile([P, HALF, PACK], BF16, name=f"z_grouped{half}", tag=f"z_grouped{half}", align_bytes=64)
+            nc.vector.tensor_copy(out=z_grouped[:], in_=z_rows[:].rearrange("p t j -> p j t"))
+            nc.vector.quantize_mx(
+                out=z_codes[:, cols].bitcast(FP8X4), scales=z_plane[:, cols], in_=z_grouped[:].rearrange("p j t -> p (j t)")
+            )
+
+        h = [keep.tile([P, S], F32, name=f"h{t}") for t in range(TILES)]
+        pages = [keep.tile([P, U], F32, name=f"page{t}") for t in range(TILES)]
+
+        def make_h(t, first, count, bank):
+            cols = slice(first, first + count)
+            piece, row = divmod(t * P, PIECE)
+            h_bank = psum.tile([P, count], F32, name=f"h_bank{t}_{first}", tag=f"bank{bank}")
+            for c in range(2):
+                picked = slice(c * PIECE + row, c * PIECE + row + P)
+                nc.tensor.matmul_mx(
+                    out=h_bank[:],
+                    lhsT=d_codes[piece][:, picked].bitcast(FP8X4),
+                    lhsT_scale=d_planes[piece][:, picked],
+                    rhs=z_codes[:, cols].bitcast(FP8X4),
+                    rhs_scale=z_plane[:, cols],
+                    start=(c == 0),
+                    stop=(c == 1),
+                )
+            nc.vector.tensor_scalar(out=h[t][:, cols], in0=h_bank[:], scalar1=0.0625, scalar2=None, op0=MULT)
+
+        def put_h(t, first, count):
+            nc.scalar.activation(
+                out=pages[t][:].indirect(entries(n2_list, first, count)), in_=h[t][:, first : first + count], func=ACT.Copy
+            )
+
+        def fetch_and_subtract(t):
+            fetched = keep.tile([P, S], F32, name=f"fetched{t}", tag=f"fetched{t}", align_bytes=64)
+            for half in range(2):
+                nc.scalar.activation(
+                    out=fetched[:, half * HALF : (half + 1) * HALF],
+                    in_=h[t][:].indirect(entries(n4_list, half * HALF, HALF)),
+                    func=ACT.Copy,
+                )
+            nw = keep.tile([P, S], F32, name=f"nw{t}")
+            nc.vector.tensor_tensor(out=nw[:], in0=h[t][:], in1=fetched[:], op=SUBTRACT)
+            return nw
+
+        def put_nw_and_store(t, nw):
+            nc.scalar.activation(out=pages[t][:].indirect(n3_list[:]), in_=nw[:], func=ACT.Copy)
+            nc.sync.dma_start(out=out[t * P : (t + 1) * P, :], in_=pages[t][:])
+
+        d_codes = [pick_d_words(0, "d_codes")]
+        for half in range(2):
+            quantise_z(half)
+            pick_d_scales(1, half, f"z_grouped{half}")
+            for t in range(2):
+                make_h(t, half * HALF, HALF, TILES + 2 * half + t)
+        place_scale_rows(nc.sync, d_planes[1])
+
+        put_h(0, 0, HALF)
+        put_h(1, 0, HALF)
+        nw = [fetch_and_subtract(0)]
+        d_codes.append(pick_d_words(1, "fetched0"))
+        for t in range(2, TILES):
+            make_h(t, 0, S, t)
+        put_h(0, HALF, HALF)
+        nw.append(fetch_and_subtract(1))
+        put_h(1, HALF, HALF)
+        put_nw_and_store(0, nw[0])
+        for t in range(2, TILES):
+            nw.append(fetch_and_subtract(t))
+            put_nw_and_store(t - 1, nw[t - 1])
+            put_h(t, 0, S)
+        put_nw_and_store(TILES - 1, nw[TILES - 1])

@@ -15,6 +15,7 @@ FP8X4 = mybir.dt.float8_e4m3fn_x4
 FP4X4 = mybir.dt.float4_e2m1fn_x4
 ACT = mybir.ActivationFunctionType
 MULT = mybir.AluOpType.mult
+ADD = mybir.AluOpType.add
 SUBTRACT = mybir.AluOpType.subtract
 
 P = 128
@@ -48,14 +49,14 @@ def tile_picked_hdaqesapagq_none_p_kernel(
             nc.sync.dma_start(offsets[:], source)
             return offsets
 
-        def load_words(source, name, tag):
-            words = keep.tile([P, source.shape[2]], I32, name=name, tag=tag, align_bytes=64)
-            nc.scalar.dma_start(out=words[:], in_=source[0].rearrange("p n r -> p (n r)").bitcast(I32))
+        def load_words(source, name):
+            words = keep.tile([P, source.shape[2]], I32, name=name, tag=name, align_bytes=64)
+            nc.sync.dma_start(out=words[:], in_=source[0].rearrange("p n r -> p (n r)").bitcast(I32))
             return words
 
-        def load_rowwise(queue, source, name):
+        def load_rowwise(source, name):
             values = keep.tile([P, PACK], F32, name=name)
-            queue.dma_start(out=values[:], in_=source.rearrange("(p t) o -> p (t o)", t=PACK))
+            nc.gpsimd.dma_start(out=values[:], in_=source.rearrange("(p t) o -> p (t o)", t=PACK))
             return values
 
         offs_list = load_list(offs, "offs_list")
@@ -63,35 +64,34 @@ def tile_picked_hdaqesapagq_none_p_kernel(
         nc.scalar.dma_start(
             out=x_bytes[:].bitcast(I32), in_=x_scales[0].bitcast(I32).unsqueeze(1).broadcast_to([16, 8, T // 4])
         )
+        w1_raw = keep.tile([P, 2 * H], U8, name="w1_raw")
+        nc.sync.dma_start(out=w1_raw[:].bitcast(I32), in_=w1_words[0].bitcast(I32))
         w1_bytes = keep.tile([P, H], U8, name="w1_bytes")
         for q in range(4):
             rows = w1_scales[0].bitcast(I32)[4 * q : 4 * q + 4, :]
             nc.sync.dma_start(
                 out=w1_bytes[:].bitcast(I32)[32 * q : 32 * (q + 1), :], in_=rows.unsqueeze(0).broadcast_to([8, 4, H // 4])
             )
-        x_table = load_words(x_words, "x_table", "x_table")
-        w1_raw = keep.tile([P, 2 * H], U8, name="w1_raw")
-        nc.sync.dma_start(out=w1_raw[:].bitcast(I32), in_=w1_words[0].bitcast(I32))
-
-        th_rows = load_rowwise(nc.gpsimd, th, "th_rows")
+        x_table = load_words(x_words, "x_table")
+        code_lists = [load_list(ka, "ka_list"), load_list(kb, "kb_list")]
         d_bytes = keep.tile([P, G], U8, name="d_bytes")
         nc.vector.memset(d_bytes[:].bitcast(I32), 0)
-        nc.gpsimd.dma_start(out=d_bytes[:].bitcast(I32)[0:P:8, :], in_=d_scales[0].bitcast(I32))
-        sl_rows = load_rowwise(nc.gpsimd, sl, "sl_rows")
-        gs_rows = load_rowwise(nc.gpsimd, gs, "gs_rows")
+        nc.sync.dma_start(out=d_bytes[:].bitcast(I32)[0:P:8, :], in_=d_scales[0].bitcast(I32))
+        sl_rows = load_rowwise(sl, "sl_rows")
+        th_rows = load_rowwise(th, "th_rows")
+        gs_rows = load_rowwise(gs, "gs_rows")
 
-        code_lists = [load_list(ka, "ka_list"), load_list(kb, "kb_list")]
+        x_picked = keep.tile([P, S], U8, name="x_picked")
+        nc.vector.tensor_copy(out=x_picked[:], in_=x_bytes[:].indirect(offs_list[:]))
+        x_plane = keep.tile([P, S], U8, name="x_plane", align_bytes=64)
+        nc.vector.tensor_copy(out=x_plane[:].bitcast(I32), in_=x_picked[:].bitcast(I32))
+        place_scale_rows(nc.sync, x_plane)
+
+        d_table = load_words(d_words, "d_table")
         n1_list = load_list(n1, "n1_list")
         n2_list = load_list(n2, "n2_list")
         n4_list = load_list(n4, "n4_list")
         n3_list = load_list(n3, "n3_list")
-
-        x_picked = keep.tile([P, S], U8, name="x_picked", tag="d_table", align_bytes=64)
-        nc.vector.tensor_copy(out=x_picked[:], in_=x_bytes[:].indirect(offs_list[:]))
-        x_plane = keep.tile([P, S], U8, name="x_plane", align_bytes=64)
-        nc.vector.tensor_copy(out=x_plane[:].bitcast(I32), in_=x_picked[:].bitcast(I32))
-        place_scale_rows(nc.scalar, x_plane)
-        d_table = load_words(d_words, "d_table", "d_table")
 
         w1_plane = keep.tile([P, H], U8, name="w1_plane", align_bytes=64)
         nc.vector.tensor_copy(
@@ -103,32 +103,28 @@ def tile_picked_hdaqesapagq_none_p_kernel(
             in_=w1_raw[:].bitcast(U16).rearrange("p (m t) -> p t m", t=PACK),
         )
         bias = keep.tile([P, PACK], F32, name="bias")
-        nc.vector.scalar_tensor_tensor(out=bias[:], in0=th_rows[:], scalar=-1.0, in1=sl_rows[:], op0=MULT, op1=MULT)
+        neg_sl = keep.tile([P, PACK], F32, name="neg_sl")
+        nc.gpsimd.tensor_scalar(out=neg_sl[:], in0=sl_rows[:], scalar1=-1.0, scalar2=0.0, op0=MULT, op1=ADD)
+        nc.gpsimd.tensor_tensor(out=bias[:], in0=neg_sl[:], in1=th_rows[:], op=MULT)
 
         x_codes = keep.tile([P, S], U32, name="x_codes", align_bytes=64)
         nc.vector.tensor_copy(out=x_codes[:], in_=x_table[:].bitcast(U32).indirect(offs_list[:]))
 
-        d_planes = [keep.tile([P, 2 * PIECE], U8, name=f"d_plane{piece}", align_bytes=64) for piece in range(2)]
+        d_picked = keep.tile([P, 2 * H], U8, name="d_picked", tag="x_table", align_bytes=64)
+        for c, code_list in enumerate(code_lists):
+            nc.vector.tensor_copy(out=d_picked[:, c * H : (c + 1) * H], in_=d_bytes[:].indirect(code_list[:]))
+        d_plane = keep.tile([P, 2 * H], U8, name="d_plane", align_bytes=64)
+        nc.vector.tensor_copy(out=d_plane[:].bitcast(I32), in_=d_picked[:].bitcast(I32))
+        place_scale_rows(nc.sync, d_plane)
 
-        def pick_d_scales(piece, c, tag):
-            picked = keep.tile([P, PIECE], U8, name=f"d_picked{piece}_{c}", tag=tag, align_bytes=64)
-            nc.vector.tensor_copy(out=picked[:], in_=d_bytes[:].indirect(entries(code_lists[c], piece * PIECE, PIECE)))
+        d_codes = {}
+
+        def pick_d_words(c, piece, tag):
+            codes = keep.tile([P, PIECE], U32, name=f"d_codes{c}_{piece}", tag=tag, align_bytes=64)
             nc.vector.tensor_copy(
-                out=d_planes[piece][:, c * PIECE : (c + 1) * PIECE].bitcast(I32), in_=picked[:].bitcast(I32)
+                out=codes[:], in_=d_table[:].bitcast(U32).indirect(entries(code_lists[c], piece * PIECE, PIECE))
             )
-
-        def pick_d_words(piece, tag):
-            codes = keep.tile([P, 2 * PIECE], U32, name=f"d_codes{piece}", tag=tag, align_bytes=64)
-            for c, code_list in enumerate(code_lists):
-                nc.vector.tensor_copy(
-                    out=codes[:, c * PIECE : (c + 1) * PIECE],
-                    in_=d_table[:].bitcast(U32).indirect(entries(code_list, piece * PIECE, PIECE)),
-                )
-            return codes
-
-        pick_d_scales(0, 0, "d_picked")
-        pick_d_scales(0, 1, "x_table")
-        place_scale_rows(nc.sync, d_planes[0])
+            d_codes[c, piece] = codes
 
         y = []
         for t in range(TILES):
@@ -143,7 +139,7 @@ def tile_picked_hdaqesapagq_none_p_kernel(
                 stop=True,
             )
             y_tile = keep.tile([P, S], F32, name=f"y{t}")
-            nc.vector.tensor_copy(out=y_tile[:], in_=y_bank[:])
+            nc.scalar.copy(out=y_tile[:], in_=y_bank[:])
             y.append(y_tile)
 
         z_codes = keep.tile([P, S], U32, name="z_codes", align_bytes=64)
@@ -151,7 +147,7 @@ def tile_picked_hdaqesapagq_none_p_kernel(
 
         def quantise_z(half):
             cols = slice(half * HALF, (half + 1) * HALF)
-            z_rows = keep.tile([P, PACK, HALF], BF16, name=f"z_rows{half}")
+            z_rows = keep.tile([P, PACK, HALF], BF16, name=f"z_rows{half}", tag="z_rows")
             for t in range(TILES):
                 sg = keep.tile([P, HALF], F32, name=f"sg{half}_{t}")
                 nc.scalar.activation(
@@ -178,11 +174,10 @@ def tile_picked_hdaqesapagq_none_p_kernel(
             piece, row = divmod(t * P, PIECE)
             h_bank = psum.tile([P, count], F32, name=f"h_bank{t}_{first}", tag=f"bank{bank}")
             for c in range(2):
-                picked = slice(c * PIECE + row, c * PIECE + row + P)
                 nc.tensor.matmul_mx(
                     out=h_bank[:],
-                    lhsT=d_codes[piece][:, picked].bitcast(FP8X4),
-                    lhsT_scale=d_planes[piece][:, picked],
+                    lhsT=d_codes[c, piece][:, row : row + P].bitcast(FP8X4),
+                    lhsT_scale=d_plane[:, c * H + t * P : c * H + (t + 1) * P],
                     rhs=z_codes[:, cols].bitcast(FP8X4),
                     rhs_scale=z_plane[:, cols],
                     start=(c == 0),
@@ -203,7 +198,7 @@ def tile_picked_hdaqesapagq_none_p_kernel(
                     in_=h[t][:].indirect(entries(n4_list, half * HALF, HALF)),
                     func=ACT.Copy,
                 )
-            nw = keep.tile([P, S], F32, name=f"nw{t}")
+            nw = keep.tile([P, S], F32, name=f"nw{t}", tag="d_table" if t == 1 else f"nw{t}", align_bytes=64)
             nc.vector.tensor_tensor(out=nw[:], in0=h[t][:], in1=fetched[:], op=SUBTRACT)
             return nw
 
@@ -211,18 +206,18 @@ def tile_picked_hdaqesapagq_none_p_kernel(
             nc.scalar.activation(out=pages[t][:].indirect(n3_list[:]), in_=nw[:], func=ACT.Copy)
             nc.sync.dma_start(out=out[t * P : (t + 1) * P, :], in_=pages[t][:])
 
-        d_codes = [pick_d_words(0, "d_codes")]
+        for c in range(2):
+            pick_d_words(c, 0, f"d_codes{c}")
         for half in range(2):
             quantise_z(half)
-            pick_d_scales(1, half, f"z_grouped{half}")
             for t in range(2):
                 make_h(t, half * HALF, HALF, TILES + 2 * half + t)
-        place_scale_rows(nc.sync, d_planes[1])
+        pick_d_words(0, 1, "z_grouped1")
 
         put_h(0, 0, HALF)
         put_h(1, 0, HALF)
         nw = [fetch_and_subtract(0)]
-        d_codes.append(pick_d_words(1, "fetched0"))
+        pick_d_words(1, 1, "fetched0")
         for t in range(2, TILES):
             make_h(t, 0, S, t)
         put_h(0, HALF, HALF)

from contextlib import ExitStack

import concourse.mybir as mybir

K, T, S, H, G, U = 512, 2048, 256, 512, 2048, 512
FLOPS = 2 * K * H * S * 3

F32 = mybir.dt.float32
BF16 = mybir.dt.bfloat16
I32 = mybir.dt.int32
U32 = mybir.dt.uint32
U16 = mybir.dt.uint16
U8 = mybir.dt.uint8
FP8X4 = mybir.dt.float8_e4m3fn_x4
FP4X4 = mybir.dt.float4_e2m1fn_x4
ACT = mybir.ActivationFunctionType
MULT = mybir.AluOpType.mult
ADD = mybir.AluOpType.add
SUBTRACT = mybir.AluOpType.subtract

P = 128
PACK = 4
TILES = H // P
HALF = S // 2
PIECE = 256
STRIPE = 16


def entries(offsets, first, count):
    return offsets[:, first // STRIPE : (first + count) // STRIPE]


def place_scale_rows(queue, plane):
    rows = plane[:].bitcast(I32)
    for j in range(1, 4):
        queue.dma_start(out=rows[j:P:32, :], in_=rows[8 * j : P : 32, :])


def tile_picked_hdaqesapagq_none_p_kernel(
    tc, x_words, x_scales, w1_words, w1_scales, sl, th, gs, d_words, d_scales, offs, n1, ka, kb, n2, n3, n4, out
):
    nc = tc.nc
    with ExitStack() as ctx:
        keep = ctx.enter_context(tc.tile_pool(name="keep", bufs=1))
        psum = ctx.enter_context(tc.psum_pool(name="psum", bufs=1))

        def load_list(source, name):
            offsets = keep.tile(list(source.shape), U16, name=name)
            nc.sync.dma_start(offsets[:], source)
            return offsets

        def load_words(source, name):
            words = keep.tile([P, source.shape[2]], I32, name=name, tag=name, align_bytes=64)
            nc.sync.dma_start(out=words[:], in_=source[0].rearrange("p n r -> p (n r)").bitcast(I32))
            return words

        def load_rowwise(source, name):
            values = keep.tile([P, PACK], F32, name=name)
            nc.gpsimd.dma_start(out=values[:], in_=source.rearrange("(p t) o -> p (t o)", t=PACK))
            return values

        offs_list = load_list(offs, "offs_list")
        x_bytes = keep.tile([P, T], U8, name="x_bytes")
        nc.scalar.dma_start(
            out=x_bytes[:].bitcast(I32), in_=x_scales[0].bitcast(I32).unsqueeze(1).broadcast_to([16, 8, T // 4])
        )
        w1_raw = keep.tile([P, 2 * H], U8, name="w1_raw")
        nc.sync.dma_start(out=w1_raw[:].bitcast(I32), in_=w1_words[0].bitcast(I32))
        w1_bytes = keep.tile([P, H], U8, name="w1_bytes")
        for q in range(4):
            rows = w1_scales[0].bitcast(I32)[4 * q : 4 * q + 4, :]
            nc.sync.dma_start(
                out=w1_bytes[:].bitcast(I32)[32 * q : 32 * (q + 1), :], in_=rows.unsqueeze(0).broadcast_to([8, 4, H // 4])
            )
        x_table = load_words(x_words, "x_table")
        code_lists = [load_list(ka, "ka_list"), load_list(kb, "kb_list")]
        d_bytes = keep.tile([P, G], U8, name="d_bytes")
        nc.vector.memset(d_bytes[:].bitcast(I32), 0)
        nc.sync.dma_start(out=d_bytes[:].bitcast(I32)[0:P:8, :], in_=d_scales[0].bitcast(I32))
        sl_rows = load_rowwise(sl, "sl_rows")
        th_rows = load_rowwise(th, "th_rows")
        gs_rows = load_rowwise(gs, "gs_rows")

        x_picked = keep.tile([P, S], U8, name="x_picked")
        nc.vector.tensor_copy(out=x_picked[:], in_=x_bytes[:].indirect(offs_list[:]))
        x_plane = keep.tile([P, S], U8, name="x_plane", align_bytes=64)
        nc.vector.tensor_copy(out=x_plane[:].bitcast(I32), in_=x_picked[:].bitcast(I32))
        place_scale_rows(nc.sync, x_plane)

        d_table = load_words(d_words, "d_table")
        n1_list = load_list(n1, "n1_list")
        n2_list = load_list(n2, "n2_list")
        n4_list = load_list(n4, "n4_list")
        n3_list = load_list(n3, "n3_list")

        w1_plane = keep.tile([P, H], U8, name="w1_plane", align_bytes=64)
        nc.vector.tensor_copy(
            out=w1_plane[:].rearrange("p (t m) -> p t m", t=PACK), in_=w1_bytes[:].rearrange("p (m t) -> p t m", t=PACK)
        )
        w1_codes = keep.tile([P, 2 * H], U8, name="w1_codes", align_bytes=64)
        nc.scalar.copy(
            out=w1_codes[:].bitcast(U16).rearrange("p (t m) -> p t m", t=PACK),
            in_=w1_raw[:].bitcast(U16).rearrange("p (m t) -> p t m", t=PACK),
        )
        bias = keep.tile([P, PACK], F32, name="bias")
        neg_sl = keep.tile([P, PACK], F32, name="neg_sl")
        nc.gpsimd.tensor_scalar(out=neg_sl[:], in0=sl_rows[:], scalar1=-1.0, scalar2=0.0, op0=MULT, op1=ADD)
        nc.gpsimd.tensor_tensor(out=bias[:], in0=neg_sl[:], in1=th_rows[:], op=MULT)

        x_codes = keep.tile([P, S], U32, name="x_codes", align_bytes=64)
        nc.vector.tensor_copy(out=x_codes[:], in_=x_table[:].bitcast(U32).indirect(offs_list[:]))

        d_picked = keep.tile([P, 2 * H], U8, name="d_picked", tag="x_table", align_bytes=64)
        for c, code_list in enumerate(code_lists):
            nc.vector.tensor_copy(out=d_picked[:, c * H : (c + 1) * H], in_=d_bytes[:].indirect(code_list[:]))
        d_plane = keep.tile([P, 2 * H], U8, name="d_plane", align_bytes=64)
        nc.vector.tensor_copy(out=d_plane[:].bitcast(I32), in_=d_picked[:].bitcast(I32))
        place_scale_rows(nc.sync, d_plane)

        d_codes = {}

        def pick_d_words(c, piece, tag):
            codes = keep.tile([P, PIECE], U32, name=f"d_codes{c}_{piece}", tag=tag, align_bytes=64)
            nc.vector.tensor_copy(
                out=codes[:], in_=d_table[:].bitcast(U32).indirect(entries(code_lists[c], piece * PIECE, PIECE))
            )
            d_codes[c, piece] = codes

        y = []
        for t in range(TILES):
            y_bank = psum.tile([P, S], F32, name=f"y_bank{t}", tag=f"bank{t}")
            nc.tensor.matmul_mx(
                out=y_bank[:],
                lhsT=w1_codes[:, 2 * P * t : 2 * P * (t + 1)].bitcast(FP4X4),
                lhsT_scale=w1_plane[:, P * t : P * (t + 1)],
                rhs=x_codes[:].bitcast(FP8X4),
                rhs_scale=x_plane[:],
                start=True,
                stop=True,
            )
            y_tile = keep.tile([P, S], F32, name=f"y{t}")
            nc.scalar.copy(out=y_tile[:], in_=y_bank[:])
            y.append(y_tile)

        z_codes = keep.tile([P, S], U32, name="z_codes", align_bytes=64)
        z_plane = keep.tile([P, S], U8, name="z_plane", align_bytes=64)

        def quantise_z(half):
            cols = slice(half * HALF, (half + 1) * HALF)
            z_rows = keep.tile([P, PACK, HALF], BF16, name=f"z_rows{half}", tag="z_rows")
            for t in range(TILES):
                sg = keep.tile([P, HALF], F32, name=f"sg{half}_{t}")
                nc.scalar.activation(
                    out=sg[:],
                    in_=y[t][:].indirect(entries(n1_list, half * HALF, HALF)),
                    func=ACT.Sigmoid,
                    scale=sl_rows[:, t : t + 1],
                    bias=bias[:, t : t + 1],
                )
                nc.vector.scalar_tensor_tensor(
                    out=z_rows[:, t, :], in0=y[t][:, cols], scalar=gs_rows[:, t : t + 1], in1=sg[:], op0=MULT, op1=MULT
                )
            z_grouped = keep.tile([P, HALF, PACK], BF16, name=f"z_grouped{half}", tag=f"z_grouped{half}", align_bytes=64)
            nc.vector.tensor_copy(out=z_grouped[:], in_=z_rows[:].rearrange("p t j -> p j t"))
            nc.vector.quantize_mx(
                out=z_codes[:, cols].bitcast(FP8X4), scales=z_plane[:, cols], in_=z_grouped[:].rearrange("p j t -> p (j t)")
            )

        h = [keep.tile([P, S], F32, name=f"h{t}") for t in range(TILES)]
        pages = [keep.tile([P, U], F32, name=f"page{t}") for t in range(TILES)]

        def make_h(t, first, count, bank):
            cols = slice(first, first + count)
            piece, row = divmod(t * P, PIECE)
            h_bank = psum.tile([P, count], F32, name=f"h_bank{t}_{first}", tag=f"bank{bank}")
            for c in range(2):
                nc.tensor.matmul_mx(
                    out=h_bank[:],
                    lhsT=d_codes[c, piece][:, row : row + P].bitcast(FP8X4),
                    lhsT_scale=d_plane[:, c * H + t * P : c * H + (t + 1) * P],
                    rhs=z_codes[:, cols].bitcast(FP8X4),
                    rhs_scale=z_plane[:, cols],
                    start=(c == 0),
                    stop=(c == 1),
                )
            nc.vector.tensor_scalar(out=h[t][:, cols], in0=h_bank[:], scalar1=0.0625, scalar2=None, op0=MULT)

        def put_h(t, first, count):
            nc.scalar.activation(
                out=pages[t][:].indirect(entries(n2_list, first, count)), in_=h[t][:, first : first + count], func=ACT.Copy
            )

        def fetch_and_subtract(t):
            fetched = keep.tile([P, S], F32, name=f"fetched{t}", tag=f"fetched{t}", align_bytes=64)
            for half in range(2):
                nc.scalar.activation(
                    out=fetched[:, half * HALF : (half + 1) * HALF],
                    in_=h[t][:].indirect(entries(n4_list, half * HALF, HALF)),
                    func=ACT.Copy,
                )
            nw = keep.tile([P, S], F32, name=f"nw{t}", tag="d_table" if t == 1 else f"nw{t}", align_bytes=64)
            nc.vector.tensor_tensor(out=nw[:], in0=h[t][:], in1=fetched[:], op=SUBTRACT)
            return nw

        def put_nw_and_store(t, nw):
            nc.scalar.activation(out=pages[t][:].indirect(n3_list[:]), in_=nw[:], func=ACT.Copy)
            nc.sync.dma_start(out=out[t * P : (t + 1) * P, :], in_=pages[t][:])

        for c in range(2):
            pick_d_words(c, 0, f"d_codes{c}")
        for half in range(2):
            quantise_z(half)
            for t in range(2):
                make_h(t, half * HALF, HALF, TILES + 2 * half + t)
        pick_d_words(0, 1, "z_grouped1")

        put_h(0, 0, HALF)
        put_h(1, 0, HALF)
        nw = [fetch_and_subtract(0)]
        pick_d_words(1, 1, "fetched0")
        for t in range(2, TILES):
            make_h(t, 0, S, t)
        put_h(0, HALF, HALF)
        nw.append(fetch_and_subtract(1))
        put_h(1, HALF, HALF)
        put_nw_and_store(0, nw[0])
        for t in range(2, TILES):
            nw.append(fetch_and_subtract(t))
            put_nw_and_store(t - 1, nw[t - 1])
            put_h(t, 0, S)
        put_nw_and_store(TILES - 1, nw[TILES - 1])
